import numpy as np
import ml_dtypes


def mxq(x, axis, fmt="e4m3"):
    dtype, down = {"e4m3": (ml_dtypes.float8_e4m3fn, 7), "e5m2": (ml_dtypes.float8_e5m2, 14)}[fmt]
    v = np.moveaxis(np.asarray(x, np.float32).astype(ml_dtypes.bfloat16).astype(np.float64), axis, -1)
    blocks = v.reshape(v.shape[:-1] + (-1, 32))
    amax = np.abs(blocks).max(-1, keepdims=True)
    byte = np.maximum(np.where(amax > 0, np.frexp(amax)[1] - 1 + 127, 0) - down, 1)
    scale = np.exp2(byte - 127.0)
    codes = (blocks / scale).astype(np.float32).astype(dtype).astype(np.float64)
    return np.moveaxis((codes * scale).reshape(v.shape), -1, axis)


WIDE = False


def mx_kscale(k):
    if not WIDE:
        return np.ones(k)
    levels = np.array([10, -10, 5, -5, 0])
    if k % 512:
        return np.exp2(np.random.permutation(np.resize(levels, k // 32))).repeat(32)
    a = np.empty((k // 512, 16))
    for p in range(k // 512):
        a[p, :8] = np.random.permutation(np.resize(levels, 8))
        for g in range(8):
            far = levels[np.abs(levels - a[p, g]) >= 10]
            a[p, g + 8] = far[np.random.randint(len(far))]
    return np.exp2(a.ravel()).repeat(32)


BF16 = ml_dtypes.bfloat16


def bf(x):
    return np.asarray(x, np.float32).astype(BF16)


def f64(x):
    return np.asarray(x).astype(np.float64)


Q, N, D, T = 1024, 1024, 512, 1024

LOG_AMPLITUDE = 8.4
DIST_SCALE = 128.0

XS = np.sqrt(4.0 * DIST_SCALE / D)


def draw0():
    s, t = mx_kscale(D), mx_kscale(N)
    x = bf(np.random.standard_normal((Q, D)) * XS * s)
    zt = bf(np.random.standard_normal((N, D)) * XS / s)
    lam = bf(np.random.uniform(0.5, 1.5, D) / (s * s))
    c = bf(np.random.standard_normal(N) * t)
    alpha = bf(np.random.standard_normal((N, T)) / np.sqrt(N) / t[:, None])
    beta = bf(np.random.standard_normal((D, T)) / (XS * np.sqrt(D)) / s[:, None])
    return {"x": x, "zt": zt, "lam": lam, "c": c, "alpha": alpha, "beta": beta}


def core(x, zt, lam, c, alpha, beta):
    x, zt, lam, c = f64(x), f64(zt), f64(lam), f64(c)
    nx = np.sum(lam[None, :] * np.square(x), axis=1)
    nz = np.sum(np.square(zt) / lam[None, :], axis=1)
    xq = mxq(x, 1, "e4m3")
    dot = xq @ mxq(zt, 1, "e4m3").T
    k = np.exp(LOG_AMPLITUDE - (nx[:, None] + nz[None, :] - 2.0 * dot) / DIST_SCALE)
    kc = k * c[None, :]
    lin = xq @ mxq(f64(beta), 0, "e4m3")
    return lin + (mxq(kc, 1, "e4m3") @ mxq(f64(alpha), 0, "e4m3"))


def e4m3fn_bytes(y):
    return np.clip(np.asarray(y, np.float64), -448.0, 448.0).astype(np.float32).astype(ml_dtypes.float8_e4m3fn).view(np.uint8)


def e4m3fn_values(b):
    return np.asarray(b, np.uint8).view(ml_dtypes.float8_e4m3fn).astype(np.float64)


def setup_inputs():
    d = draw0()
    x0 = np.asarray(d['alpha']).astype(np.float64)
    s = (np.max(np.abs(x0), axis=(1,), keepdims=True) / 448.0).astype(np.float32)
    out = {}
    for k, v in d.items():
        if k == 'alpha':
            out['alpha_bytes'] = e4m3fn_bytes(x0 / s.astype(np.float64))
            out['alpha_scale'] = s
        else:
            out[k] = v
    return out


def reference(x, zt, lam, c, alpha_bytes, alpha_scale, beta):
    return core(x, zt, lam, c, e4m3fn_values(alpha_bytes) * alpha_scale.astype(np.float64), beta)

@@ -1,0 +1,306 @@
+from contextlib import ExitStack
+
+import concourse.mybir as mybir
+from concourse.masks import make_identity
+
+Q, N, D, T = 1024, 1024, 512, 1024
+FLOPS = 2 * (Q * N * D + Q * D * T + Q * N * T)
+
+F32 = mybir.dt.float32
+BF16 = mybir.dt.bfloat16
+U32 = mybir.dt.uint32
+U8 = mybir.dt.uint8
+FP8 = mybir.dt.float8_e4m3fn
+FP8X4 = mybir.dt.float8_e4m3fn_x4
+ALU = mybir.AluOpType
+ACT = mybir.ActivationFunctionType
+
+P = 128
+HALF = 512
+LOG_AMPLITUDE = 8.4
+DIST_SCALE = 128.0
+LN_LOW = 2.0**-63
+LN_HIGH = 2.0**63
+CHUNKS = ((0, 512), (512, 256), (768, 256))
+
+ORDER = (
+    "DX:V Tz0:P ZC:V Tx0:P Cz0:S Tz1:P Cx0:V LN:S Tz2:P DZ:V Yx00:P Yx01:P "
+    "Cz2:V Ax00:V Yz01:P Cz1:S Qz2:V Tx1:P Ax01:V Az01:S Yz10:P Qz1:V Cx1:S MB1:V "
+    "Yz20:P Az10:S Yx10:P Bx0:P Az20:S Yz11:P Qx1:V Xx0:S Ax10:V Yz21:P WA010:S QB1:V "
+    "Yx11:P Yz00:P Ax11:V Az11:S L031:P L021:P Qz0:V Az00:S Bx1:P Fz1:V Qx0:V Tz3:P "
+    "Az21:S MB0:V L011:P Xx1:S D002:P Cz3:S L001:P D010:P Fz2:V WA000:S Fz0:V D003:P "
+    "f002:V Yz30:P f010:V Yz31:P Az30:S f003:V D011:P Az31:S Qz3:V D000:P f011:V Tx2:P "
+    "WA001:S f000:V D012:P Tx3:P Fz3:V QB0:V Cx2:S D001:P f012:V Cx3:S Yx21:P MA00:V "
+    "WA110:S Yx20:P Yx30:P WA011:S f001:V Ax20:V Yx31:P E00:S Ax21:V D013:P MA01:V Bx2:P "
+    "f013:V Xx2:S QA01:V WA111:S Qx2:V K00:V D100:P E01:S D112:P MA11:V G011:P G031:P "
+    "G021:P G001:P f100:V QA11:V WA101:S D110:P K01:V f110:V WA100:S H021:P H001:P Ax31:V "
+    "H011:P H031:P QA00:V O001:S D102:P O011:S MA10:V L000:P G000:P O031:S L010:P G010:P "
+    "O021:S f102:V L030:P G030:P L020:P QA10:V E10:S G020:P Ax30:V H020:P H030:P Qx3:V "
+    "H010:P O020:S f112:V Bx3:P D200:P O030:S D212:P Xx3:V L101:P K10:V E11:S D202:P "
+    "f212:V L110:P G101:P f200:V G110:P O010:S H000:P f202:V D210:P O000:S K11:V L100:P "
+    "G100:P f210:V E20:S H110:P L111:P O110:V H100:P G111:P E21:S O100:V H111:P L211:P "
+    "K20:V H101:P O111:V L201:P G211:P O101:S K21:V G201:P L210:P H211:P G210:P O211:S "
+    "H201:P H210:P O201:S L200:P O210:V G200:P H200:P O200:V "
+)
+
+
+def tile_ardgaussianprocessmean_kernel(tc, x, zt, lam, c, alpha_bytes, alpha_scale, beta, out):
+    nc = tc.nc
+    with ExitStack() as ctx:
+        keep = ctx.enter_context(tc.tile_pool(name="keep", bufs=1))
+        outs = ctx.enter_context(tc.tile_pool(name="outs", bufs=8))
+        psum = ctx.enter_context(tc.psum_pool(name="psum", bufs=4))
+        ctx.enter_context(tc.manual_schedule())
+
+        def keep_tile(shape, dtype, label):
+            t = keep.tile(shape, dtype, name=label, tag=label, align_bytes=64)
+            return t
+
+        source = {"z": zt.rearrange("(h m t) d -> h m t d", m=P, t=4), "x": x.rearrange("(h m t) d -> h m t d", m=P, t=4)}
+        rows = {}
+        beta_rows = keep_tile([P, 4, T], BF16, "beta_rows")
+        code_rows = [keep_tile([P, 4, T], U8, f"code_rows{g}") for g in range(2)]
+        codes_src = alpha_bytes.rearrange("(g p t) w -> g p t w", p=P, t=4)
+
+        def load_rows(kind, b):
+            rows[kind, b] = keep_tile([P, 2, D], BF16, f"rows_{kind}{b}")
+            s = 2 * (b % 2)
+            nc.sync.dma_start(out=rows[kind, b][:], in_=source[kind][b // 2][:, s : s + 2, :])
+
+        for what in "z0 x0 z1 z2 z3 x1 be a0 a1 x2 x3".split(" "):
+            if what == "be":
+                nc.sync.dma_start(out=beta_rows[:], in_=beta.rearrange("(p t) w -> p t w", t=4))
+            elif what[0] == "a":
+                g = int(what[1])
+                nc.sync.dma_start(out=code_rows[g][:], in_=codes_src[g])
+            else:
+                load_rows(what[0], int(what[1]))
+
+        lam_b = keep_tile([P, 4], BF16, "lam_b")
+        c_b = keep_tile([P, 2, 4], BF16, "c_b")
+        scale_in = keep_tile([P, 2, 4], F32, "scale_in")
+        nc.scalar.dma_start(out=lam_b[:], in_=lam.rearrange("(p t) -> p t", t=4))
+        nc.scalar.dma_start(out=c_b[:], in_=c.rearrange("(g p t) -> p g t", p=P, t=4))
+        nc.scalar.dma_start(out=scale_in[:], in_=alpha_scale.rearrange("(g p t) o -> p g (t o)", p=P, t=4))
+
+        one = keep_tile([P, 1], F32, "one")
+        warm = keep_tile([P, 1], F32, "warm")
+        nc.vector.memset(one[:], 1.0)
+        nc.scalar.activation(warm[:], one[:], ACT.Ln)
+        ident = keep_tile([P, P], F32, "ident")
+        make_identity(nc, ident[:])
+
+        ident_b = keep_tile([P, P], BF16, "ident_b")
+        make_identity(nc, ident_b[:])
+        power = keep_tile([P, 4], F32, "power")
+        nc.gpsimd.memset(power[:], -0.5)
+        root = keep_tile([P, 4], F32, "root")
+        root_b = keep_tile([P, 4], BF16, "root_b")
+        root_hi = keep_tile([P, 4], F32, "root_hi")
+        root_lo = keep_tile([P, 4], F32, "root_lo")
+        nc.gpsimd.tensor_scalar(root[:], lam_b[:], 2.0, 0.0, ALU.mult, ALU.add)
+        nc.gpsimd.tensor_tensor(root[:], root[:], power[:], ALU.pow)
+        nc.gpsimd.tensor_copy(out=root_b[:], in_=root[:])
+        nc.gpsimd.tensor_copy(out=root_hi[:], in_=root_b[:])
+        nc.gpsimd.tensor_tensor(root_lo[:], root[:], root_hi[:], ALU.subtract)
+        diag_x = keep_tile([P, 4, P], BF16, "diag_x")
+        diag_z = keep_tile([P, 2, 4, P], BF16, "diag_z")
+        sign = keep_tile([P, 8], F32, "sign")
+        c_abs = keep_tile([P, 8], F32, "c_abs")
+        ln_in = keep_tile([P, 2, 8], F32, "ln_in")
+        ln_out = keep_tile([P, 2, 8], F32, "ln_out")
+        c_rec = keep_tile([P, 8], F32, "c_rec")
+        offset = keep_tile([P, 8], F32, "offset")
+        scale = keep_tile([P, 8], F32, "scale")
+        c_flat = c_b[:].rearrange("p g t -> p (g t)")
+
+        def c_chain():
+            nc.vector.tensor_scalar(sign[:], c_flat, 0.0, 2.0, ALU.is_ge, ALU.mult)
+            nc.vector.tensor_scalar(sign[:], sign[:], -1.0, None, ALU.add)
+            nc.vector.tensor_tensor(c_abs[:], c_flat, sign[:], ALU.mult)
+            nc.vector.tensor_scalar(ln_in[:, 0, :], c_abs[:], LN_LOW, LN_HIGH, ALU.max, ALU.min)
+            nc.vector.reciprocal(c_rec[:], ln_in[:, 0, :])
+            nc.vector.tensor_tensor(c_rec[:], c_abs[:], c_rec[:], ALU.mult)
+            nc.vector.tensor_scalar(ln_in[:, 1, :], c_rec[:], LN_LOW, 2.0 * LN_HIGH, ALU.max, ALU.min)
+
+        def logs():
+            nc.gpsimd.tensor_tensor(scale[:], scale_in[:].rearrange("p g t -> p (g t)"), sign[:], ALU.mult)
+            nc.scalar.activation(ln_out[:], ln_in[:], ACT.Ln)
+            nc.scalar.activation(warm[:], one[:], ACT.Exp)
+            nc.gpsimd.tensor_tensor(offset[:], ln_out[:, 0, :], ln_out[:, 1, :], ALU.add)
+            nc.gpsimd.tensor_scalar(offset[:], offset[:], -DIST_SCALE / 2, -DIST_SCALE / 2 * LOG_AMPLITUDE, ALU.mult, ALU.add)
+
+        turned, codes, planes = {}, {}, {}
+        for kind in "zx":
+            turned[kind] = keep_tile([P, 1024, 4], BF16, "turned_" + kind)
+            codes[kind] = keep_tile([P, 1024], U32, "codes_" + kind)
+            planes[kind] = keep_tile([P, 1024], U8, "planes_" + kind)
+        nz = keep_tile([P, 8], F32, "nz")
+        nz_half = keep_tile([P, 8], F32, "nz_half")
+        junk_s = keep_tile([P, D], BF16, "junk_s")
+        junk_v = keep_tile([P, D], BF16, "junk_v")
+        nx_col = keep_tile([P, 8], F32, "nx_col")
+        nx = keep_tile([P, Q], F32, "nx")
+        bq = keep_tile([P, T], U32, "bq")
+        bs = keep_tile([P, T], U8, "bs")
+        aq = [keep_tile([P, T], U32, f"aq{g}") for g in range(2)]
+        a_s = [keep_tile([P, T], U8, f"as{g}") for g in range(2)]
+        bank, sq, wide, mixed, dist, kern, kq, ks = {}, {}, {}, {}, {}, {}, {}, {}
+        out_view = out.rearrange("(h m j) w -> h j m w", m=P, j=4)
+
+        def move(engine, dst, src):
+            if engine == "V":
+                nc.vector.tensor_copy(out=dst, in_=src)
+            else:
+                nc.scalar.copy(dst, src)
+
+        def cols(b, n=256):
+            return slice(n * b, n * b + n)
+
+        def mm(o, l, ls, r, rs, start, stop):
+            nc.tensor.matmul_mx(out=o, lhsT=l.bitcast(FP8X4), lhsT_scale=ls, rhs=r.bitcast(FP8X4), rhs_scale=rs, start=start, stop=stop)
+
+        def mix(dst, src):
+            nc.vector.tensor_copy(out=dst, in_=src)
+
+        for step in ORDER.split():
+            name, e = step.split(":")
+            o = name[0]
+            if o == "T":
+                k, b = name[1], int(name[2])
+                t = psum.tile([P, 2, 2, P], F32, tag="w", bufs=4)
+                for r in range(2):
+                    view = rows[k, b][:, r, :].bitcast(F32)
+                    for u in range(2):
+                        nc.tensor.transpose(t[:, r, u, :], view[:, u : D // 2 : 2], ident[:])
+                bank["T", k, b] = t
+            elif o == "C":
+                k, b = name[1], int(name[2])
+                move(e, turned[k][:, cols(b), :].bitcast(F32).rearrange("p (r m) u -> p r m u", m=P), bank["T", k, b][:].rearrange("p r u m -> p r m u"))
+            elif name == "ZC":
+                c_chain()
+            elif name == "LN":
+                logs()
+            elif name == "DX":
+                for t in range(4):
+                    nc.vector.tensor_scalar(diag_x[:, t, :], ident_b[:], lam_b[:, t : t + 1], None, ALU.mult)
+            elif name == "DZ":
+                for v, part in enumerate((root_hi, root_lo)):
+                    for t in range(4):
+                        nc.vector.tensor_scalar(diag_z[:, v, t, :], ident_b[:], part[:, t : t + 1], None, ALU.mult)
+            elif o == "Q" and name[1] in "xz":
+                k, b = name[1], int(name[2])
+                nc.vector.quantize_mx(out=codes[k][:, cols(b)].bitcast(FP8X4), scales=planes[k][:, cols(b)], in_=turned[k][:, cols(b), :].rearrange("p n t -> p (n t)"))
+            elif o == "Y":
+                k, b, r = name[1], int(name[2]), int(name[3])
+                y = psum.tile([P, 4, P], F32, tag="w", bufs=4)
+                for t in range(4):
+                    left = turned[k][:, 256 * b + P * r : 256 * b + P * r + P, t]
+                    if k == "x":
+                        nc.tensor.matmul(y[:, t, :], lhsT=left, rhs=diag_x[:, t, :], start=True, stop=True)
+                    else:
+                        for v in range(2):
+                            nc.tensor.matmul(y[:, t, :], lhsT=left, rhs=diag_z[:, v, t, :], start=(v == 0), stop=(v == 1))
+                bank["Y", k, b, r] = y
+            elif o == "A":
+                k, b, r = name[1], int(name[2]), int(name[3])
+                y = bank["Y", k, b, r]
+                j = 2 * b + r
+                if k == "z":
+                    nc.scalar.activation(junk_s[:], y[:].rearrange("p t n -> p (t n)"), ACT.Square, accum_out=nz_half[:, j : j + 1])
+                else:
+                    nc.vector.scalar_tensor_tensor(
+                        junk_v[:].rearrange("p (t n) -> p t n", t=4),
+                        y[:],
+                        0.5,
+                        rows[k, b][:, r, :].rearrange("p (n t) -> p t n", t=4),
+                        ALU.mult,
+                        ALU.mult,
+                        accum_out=nx_col[:, j : j + 1],
+                    )
+            elif o == "F":
+                b = int(name[2])
+                nc.vector.tensor_tensor(nz[:, cols(b, 2)], nz_half[:, cols(b, 2)], offset[:, cols(b, 2)], ALU.add)
+            elif o == "B":
+                b = int(name[2])
+                t = psum.tile([P, HALF], F32, tag="w", bufs=4)
+                for j in range(2):
+                    nc.tensor.transpose(t[:, P * j : P * j + P], nx_col[:, 2 * b + j : 2 * b + j + 1].to_broadcast([P, P]), ident[:])
+                bank["B", b] = t
+            elif o == "X":
+                b = int(name[2])
+                move(e, nx[:, cols(b)], bank["B", b][:, 0:256])
+            elif name[:2] == "MB":
+                w = int(name[2])
+                mixed["b", w] = keep_tile([P, HALF, 4], BF16, f"mixb{w}")
+                v = beta_rows[:, :, cols(w, HALF)].rearrange("p t n -> p n t")
+                if e == "G":
+                    nc.gpsimd.tensor_scalar(mixed["b", w][:], v, 1.0, 0.0, ALU.mult, ALU.add)
+                else:
+                    mix(mixed["b", w][:], v)
+            elif name[:2] == "QB":
+                w = int(name[2])
+                s = cols(w, HALF)
+                nc.vector.quantize_mx(out=bq[:, s].bitcast(FP8X4), scales=bs[:, s], in_=mixed["b", w][:].rearrange("p n t -> p (n t)"))
+            elif name[:2] == "WA":
+                g, w, k = int(name[2]), int(name[3]), int(name[4])
+                if (g, w) not in wide:
+                    wide[g, w] = keep_tile([P, 4, HALF], BF16, f"wide{g}{w}")
+                for j in (2 * k, 2 * k + 1):
+                    v = code_rows[g][:, j, cols(w, HALF)].bitcast(FP8)
+                    one_col = scale[:, 4 * g + j : 4 * g + j + 1]
+                    if e == "V":
+                        nc.vector.tensor_scalar(wide[g, w][:, j, :], v, one_col, None, ALU.mult)
+                    else:
+                        nc.scalar.activation(wide[g, w][:, j, :], v, ACT.Copy, scale=one_col)
+            elif name[:2] == "MA":
+                g, w = int(name[2]), int(name[3])
+                mixed[g, w] = keep_tile([P, HALF, 4], BF16, f"mix{g}{w}")
+                mix(mixed[g, w][:], wide[g, w][:].rearrange("p t n -> p n t"))
+            elif name[:2] == "QA":
+                g, w = int(name[2]), int(name[3])
+                s = cols(w, HALF)
+                nc.vector.quantize_mx(out=aq[g][:, s].bitcast(FP8X4), scales=a_s[g][:, s], in_=mixed[g, w][:].rearrange("p n t -> p (n t)"))
+            elif o == "D":
+                i, g, t0 = int(name[1]), int(name[2]), int(name[3])
+                q0, width = CHUNKS[i]
+                t = psum.tile([P, HALF], F32, tag="w", bufs=4)
+                for s in range(HALF // width):
+                    zc = cols(4 * g + t0 + s, P)
+                    qc = slice(q0, q0 + width)
+                    mm(t[:, cols(s, width)], codes["z"][:, zc], planes["z"][:, zc], codes["x"][:, qc], planes["x"][:, qc], True, True)
+                bank["D", i, g, t0] = t
+            elif o == "f":
+                i, g, t0 = int(name[1]), int(name[2]), int(name[3])
+                q0, width = CHUNKS[i]
+                if (i, g) not in dist:
+                    dist[i, g] = keep_tile([P, 4, width], F32, f"dist{i}{g}")
+                for s in range(HALF // width):
+                    j = 4 * g + t0 + s
+                    nc.vector.scalar_tensor_tensor(dist[i, g][:, t0 + s, :], bank["D", i, g, t0][:, cols(s, width)], nz[:, j : j + 1], nx[:, q0 : q0 + width], ALU.subtract, ALU.subtract)
+            elif o == "E":
+                i, g = int(name[1]), int(name[2])
+                kern[i, g] = keep_tile([P, CHUNKS[i][1], 4], BF16, f"kern{i}{g}")
+                nc.scalar.activation(kern[i, g][:], dist[i, g][:].rearrange("p t n -> p n t"), ACT.Exp, scale=2.0 / DIST_SCALE)
+            elif o == "K":
+                i, g = int(name[1]), int(name[2])
+                width = CHUNKS[i][1]
+                kq[i, g] = keep_tile([P, width], U32, f"kq{i}{g}")
+                ks[i, g] = keep_tile([P, width], U8, f"ks{i}{g}")
+                nc.vector.quantize_mx(out=kq[i, g][:].bitcast(FP8X4), scales=ks[i, g][:], in_=kern[i, g][:].rearrange("p n t -> p (n t)"))
+            else:
+                i, b, w = int(name[1]), int(name[2]), int(name[3])
+                q0 = CHUNKS[i][0] + P * b
+                s = cols(w, HALF)
+                if o == "L":
+                    t = psum.tile([P, HALF], F32, tag="acc", bufs=4)
+                    bank["A", i, b, w] = t
+                    qc = slice(q0, q0 + P)
+                    mm(t[:], codes["x"][:, qc], planes["x"][:, qc], bq[:, s], bs[:, s], True, False)
+                elif o in "GH":
+                    g = "GH".index(o)
+                    mm(bank["A", i, b, w][:], kq[i, g][:, cols(b, P)], ks[i, g][:, cols(b, P)], aq[g][:, s], a_s[g][:, s], False, g == 1)
+                else:
+                    t = outs.tile([P, HALF], F32, tag="res")
+                    move(e, t[:], bank["A", i, b, w][:])
+                    nc.sync.dma_start(out=out_view[q0 // HALF, (q0 % HALF) // P, :, s], in_=t[:])

@@ -24,23 +24,23 @@ LN_HIGH = 2.0**63
 CHUNKS = ((0, 512), (512, 256), (768, 256))
 
 ORDER = (
-    "DX:V Tz0:P ZC:V Tx0:P Cz0:S Tz1:P Cx0:V LN:S Tz2:P DZ:V Yx00:P Yx01:P "
-    "Cz2:V Ax00:V Yz01:P Cz1:S Qz2:V Tx1:P Ax01:V Az01:S Yz10:P Qz1:V Cx1:S MB1:V "
-    "Yz20:P Az10:S Yx10:P Bx0:P Az20:S Yz11:P Qx1:V Xx0:S Ax10:V Yz21:P WA010:S QB1:V "
-    "Yx11:P Yz00:P Ax11:V Az11:S L031:P L021:P Qz0:V Az00:S Bx1:P Fz1:V Qx0:V Tz3:P "
-    "Az21:S MB0:V L011:P Xx1:S D002:P Cz3:S L001:P D010:P Fz2:V WA000:S Fz0:V D003:P "
-    "f002:V Yz30:P f010:V Yz31:P Az30:S f003:V D011:P Az31:S Qz3:V D000:P f011:V Tx2:P "
-    "WA001:S f000:V D012:P Tx3:P Fz3:V QB0:V Cx2:S D001:P f012:V Cx3:S Yx21:P MA00:V "
-    "WA110:S Yx20:P Yx30:P WA011:S f001:V Ax20:V Yx31:P E00:S Ax21:V D013:P MA01:V Bx2:P "
-    "f013:V Xx2:S QA01:V WA111:S Qx2:V K00:V D100:P E01:S D112:P MA11:V G011:P G031:P "
-    "G021:P G001:P f100:V QA11:V WA101:S D110:P K01:V f110:V WA100:S H021:P H001:P Ax31:V "
-    "H011:P H031:P QA00:V O001:S D102:P O011:S MA10:V L000:P G000:P O031:S L010:P G010:P "
-    "O021:S f102:V L030:P G030:P L020:P QA10:V E10:S G020:P Ax30:V H020:P H030:P Qx3:V "
-    "H010:P O020:S f112:V Bx3:P D200:P O030:S D212:P Xx3:V L101:P K10:V E11:S D202:P "
-    "f212:V L110:P G101:P f200:V G110:P O010:S H000:P f202:V D210:P O000:S K11:V L100:P "
-    "G100:P f210:V E20:S H110:P L111:P O110:V H100:P G111:P E21:S O100:V H111:P L211:P "
-    "K20:V H101:P O111:V L201:P G211:P O101:S K21:V G201:P L210:P H211:P G210:P O211:S "
-    "H201:P H210:P O201:S L200:P O210:V G200:P H200:P O200:V "
+    "DX:V Tz0:P ZC:V Tx0:P Cz0:S Tz1:P Cx0:S Qz0:V Tz2:P DZ:V LN:S Yx01:P "
+    "Cz1:V Tx1:P Ax01:V Yz01:P Qz1:V Cx1:S Qx0:V Yz11:P Cz2:S MB0:V Yx11:P Az01:S "
+    "Yz20:P Az11:S Yz00:P Ax11:V Az20:S Yz10:P QB0:V Az00:S Yx00:P WA111:V Yx10:P WA101:S "
+    "L010:P Ax00:V L000:P Yz21:P Ax10:V Az10:S Bx0:P Fz0:V Qz2:V Az21:S Bx1:P Fz1:V "
+    "Tz3:P Qx1:V Xx1:S MB1:V Xx0:S D010:P WA010:S D000:P D003:P Fz2:V L030:P f000:V "
+    "L020:P Cz3:S f003:V D001:P WA100:S f010:V Yz31:P f001:V D011:P Az31:S D002:P QB1:V "
+    "Yz30:P WA000:S f011:V Tx3:P f002:V Az30:S Tx2:P MA10:V Cx3:S Cx2:S Fz3:V Yx31:P "
+    "Qz3:V WA011:S Yx30:P QA10:V D013:P Ax30:V D012:P WA110:S f013:V Yx20:P MA01:V Yx21:P "
+    "WA001:S Ax20:V E00:S MA00:V f012:V QA00:V E01:S Qx2:V K00:V D112:P D102:P Ax31:V "
+    "G010:P G020:P Ax21:V G000:P Bx3:P QA01:V G030:P Xx3:S Bx2:P K01:V D100:P Xx2:S "
+    "MA11:V H000:P H020:P O000:S H030:P H010:P f102:V O020:S D110:P L021:P f100:V O010:S "
+    "G021:P L011:P f110:V O030:S G011:P L031:P E10:S QA11:V G031:P L001:P f112:V G001:P "
+    "H031:P H001:P Qx3:V O031:S H021:P K10:V H011:P O001:V E11:S D202:P L100:P f202:V "
+    "D200:P L101:P G101:P f200:V O021:S D210:P D212:P K11:V O011:S G100:P f210:V L111:P "
+    "E20:S H101:P f212:V L110:P G110:P O101:V H110:P E21:S H100:P K20:V G111:P O110:V "
+    "H111:P L211:P O100:V G211:P O111:S L200:P K21:V G200:P L201:P H200:P H211:P O200:S "
+    "G201:P O211:V H201:P L210:P O201:S G210:P H210:P O210:S "
 )
 
 
@@ -161,7 +161,7 @@ def tile_ardgaussianprocessmean_kernel(tc, x, zt, lam, c, alpha_bytes, alpha_sca
             nc.tensor.matmul_mx(out=o, lhsT=l.bitcast(FP8X4), lhsT_scale=ls, rhs=r.bitcast(FP8X4), rhs_scale=rs, start=start, stop=stop)
 
         def mix(dst, src):
-            nc.vector.tensor_copy(out=dst, in_=src)
+            nc.vector.tensor_copy(out=dst.rearrange("p (n i) t -> p n t i", i=4), in_=src.rearrange("p t (n i) -> p n t i", i=4))
 
         for step in ORDER.split():
             name, e = step.split(":")
@@ -233,11 +233,8 @@ def tile_ardgaussianprocessmean_kernel(tc, x, zt, lam, c, alpha_bytes, alpha_sca
             elif name[:2] == "MB":
                 w = int(name[2])
                 mixed["b", w] = keep_tile([P, HALF, 4], BF16, f"mixb{w}")
-                v = beta_rows[:, :, cols(w, HALF)].rearrange("p t n -> p n t")
-                if e == "G":
-                    nc.gpsimd.tensor_scalar(mixed["b", w][:], v, 1.0, 0.0, ALU.mult, ALU.add)
-                else:
-                    mix(mixed["b", w][:], v)
+                v = beta_rows[:, :, cols(w, HALF)]
+                mix(mixed["b", w][:], v)
             elif name[:2] == "QB":
                 w = int(name[2])
                 s = cols(w, HALF)
@@ -256,7 +253,7 @@ def tile_ardgaussianprocessmean_kernel(tc, x, zt, lam, c, alpha_bytes, alpha_sca
             elif name[:2] == "MA":
                 g, w = int(name[2]), int(name[3])
                 mixed[g, w] = keep_tile([P, HALF, 4], BF16, f"mix{g}{w}")
-                mix(mixed[g, w][:], wide[g, w][:].rearrange("p t n -> p n t"))
+                mix(mixed[g, w][:], wide[g, w][:])
             elif name[:2] == "QA":
                 g, w = int(name[2]), int(name[3])
                 s = cols(w, HALF)
@@ -281,7 +278,7 @@ def tile_ardgaussianprocessmean_kernel(tc, x, zt, lam, c, alpha_bytes, alpha_sca
             elif o == "E":
                 i, g = int(name[1]), int(name[2])
                 kern[i, g] = keep_tile([P, CHUNKS[i][1], 4], BF16, f"kern{i}{g}")
-                nc.scalar.activation(kern[i, g][:], dist[i, g][:].rearrange("p t n -> p n t"), ACT.Exp, scale=2.0 / DIST_SCALE)
+                nc.scalar.activation(kern[i, g][:].rearrange("p (n i) t -> p n t i", i=4), dist[i, g][:].rearrange("p t (n i) -> p n t i", i=4), ACT.Exp, scale=2.0 / DIST_SCALE)
             elif o == "K":
                 i, g = int(name[1]), int(name[2])
                 width = CHUNKS[i][1]

from contextlib import ExitStack

import concourse.mybir as mybir
from concourse.masks import make_identity

Q, N, D, T = 1024, 1024, 512, 1024
FLOPS = 2 * (Q * N * D + Q * D * T + Q * N * T)

F32 = mybir.dt.float32
BF16 = mybir.dt.bfloat16
U32 = mybir.dt.uint32
U8 = mybir.dt.uint8
FP8 = mybir.dt.float8_e4m3fn
FP8X4 = mybir.dt.float8_e4m3fn_x4
ALU = mybir.AluOpType
ACT = mybir.ActivationFunctionType

P = 128
HALF = 512
LOG_AMPLITUDE = 8.4
DIST_SCALE = 128.0
LN_LOW = 2.0**-63
LN_HIGH = 2.0**63
CHUNKS = ((0, 512), (512, 256), (768, 256))

ORDER = (
    "DX:V Tz0:P ZC:V Tx0:P Cz0:S Tz1:P Cx0:S Qz0:V Tz2:P DZ:V LN:S Yx01:P "
    "Cz1:V Tx1:P Ax01:V Yz01:P Qz1:V Cx1:S Qx0:V Yz11:P Cz2:S MB0:V Yx11:P Az01:S "
    "Yz20:P Az11:S Yz00:P Ax11:V Az20:S Yz10:P QB0:V Az00:S Yx00:P WA111:V Yx10:P WA101:S "
    "L010:P Ax00:V L000:P Yz21:P Ax10:V Az10:S Bx0:P Fz0:V Qz2:V Az21:S Bx1:P Fz1:V "
    "Tz3:P Qx1:V Xx1:S MB1:V Xx0:S D010:P WA010:S D000:P D003:P Fz2:V L030:P f000:V "
    "L020:P Cz3:S f003:V D001:P WA100:S f010:V Yz31:P f001:V D011:P Az31:S D002:P QB1:V "
    "Yz30:P WA000:S f011:V Tx3:P f002:V Az30:S Tx2:P MA10:V Cx3:S Cx2:S Fz3:V Yx31:P "
    "Qz3:V WA011:S Yx30:P QA10:V D013:P Ax30:V D012:P WA110:S f013:V Yx20:P MA01:V Yx21:P "
    "WA001:S Ax20:V E00:S MA00:V f012:V QA00:V E01:S Qx2:V K00:V D112:P D102:P Ax31:V "
    "G010:P G020:P Ax21:V G000:P Bx3:P QA01:V G030:P Xx3:S Bx2:P K01:V D100:P Xx2:S "
    "MA11:V H000:P H020:P O000:S H030:P H010:P f102:V O020:S D110:P L021:P f100:V O010:S "
    "G021:P L011:P f110:V O030:S G011:P L031:P E10:S QA11:V G031:P L001:P f112:V G001:P "
    "H031:P H001:P Qx3:V O031:S H021:P K10:V H011:P O001:V E11:S D202:P L100:P f202:V "
    "D200:P L101:P G101:P f200:V O021:S D210:P D212:P K11:V O011:S G100:P f210:V L111:P "
    "E20:S H101:P f212:V L110:P G110:P O101:V H110:P E21:S H100:P K20:V G111:P O110:V "
    "H111:P L211:P O100:V G211:P O111:S L200:P K21:V G200:P L201:P H200:P H211:P O200:S "
    "G201:P O211:V H201:P L210:P O201:S G210:P H210:P O210:S "
)


def tile_ardgaussianprocessmean_kernel(tc, x, zt, lam, c, alpha_bytes, alpha_scale, beta, out):
    nc = tc.nc
    with ExitStack() as ctx:
        keep = ctx.enter_context(tc.tile_pool(name="keep", bufs=1))
        outs = ctx.enter_context(tc.tile_pool(name="outs", bufs=8))
        psum = ctx.enter_context(tc.psum_pool(name="psum", bufs=4))
        ctx.enter_context(tc.manual_schedule())

        def keep_tile(shape, dtype, label):
            t = keep.tile(shape, dtype, name=label, tag=label, align_bytes=64)
            return t

        source = {"z": zt.rearrange("(h m t) d -> h m t d", m=P, t=4), "x": x.rearrange("(h m t) d -> h m t d", m=P, t=4)}
        rows = {}
        beta_rows = keep_tile([P, 4, T], BF16, "beta_rows")
        code_rows = [keep_tile([P, 4, T], U8, f"code_rows{g}") for g in range(2)]
        codes_src = alpha_bytes.rearrange("(g p t) w -> g p t w", p=P, t=4)

        def load_rows(kind, b):
            rows[kind, b] = keep_tile([P, 2, D], BF16, f"rows_{kind}{b}")
            s = 2 * (b % 2)
            nc.sync.dma_start(out=rows[kind, b][:], in_=source[kind][b // 2][:, s : s + 2, :])

        for what in "z0 x0 z1 z2 z3 x1 be a0 a1 x2 x3".split(" "):
            if what == "be":
                nc.sync.dma_start(out=beta_rows[:], in_=beta.rearrange("(p t) w -> p t w", t=4))
            elif what[0] == "a":
                g = int(what[1])
                nc.sync.dma_start(out=code_rows[g][:], in_=codes_src[g])
            else:
                load_rows(what[0], int(what[1]))

        lam_b = keep_tile([P, 4], BF16, "lam_b")
        c_b = keep_tile([P, 2, 4], BF16, "c_b")
        scale_in = keep_tile([P, 2, 4], F32, "scale_in")
        nc.scalar.dma_start(out=lam_b[:], in_=lam.rearrange("(p t) -> p t", t=4))
        nc.scalar.dma_start(out=c_b[:], in_=c.rearrange("(g p t) -> p g t", p=P, t=4))
        nc.scalar.dma_start(out=scale_in[:], in_=alpha_scale.rearrange("(g p t) o -> p g (t o)", p=P, t=4))

        one = keep_tile([P, 1], F32, "one")
        warm = keep_tile([P, 1], F32, "warm")
        nc.vector.memset(one[:], 1.0)
        nc.scalar.activation(warm[:], one[:], ACT.Ln)
        ident = keep_tile([P, P], F32, "ident")
        make_identity(nc, ident[:])

        ident_b = keep_tile([P, P], BF16, "ident_b")
        make_identity(nc, ident_b[:])
        power = keep_tile([P, 4], F32, "power")
        nc.gpsimd.memset(power[:], -0.5)
        root = keep_tile([P, 4], F32, "root")
        root_b = keep_tile([P, 4], BF16, "root_b")
        root_hi = keep_tile([P, 4], F32, "root_hi")
        root_lo = keep_tile([P, 4], F32, "root_lo")
        nc.gpsimd.tensor_scalar(root[:], lam_b[:], 2.0, 0.0, ALU.mult, ALU.add)
        nc.gpsimd.tensor_tensor(root[:], root[:], power[:], ALU.pow)
        nc.gpsimd.tensor_copy(out=root_b[:], in_=root[:])
        nc.gpsimd.tensor_copy(out=root_hi[:], in_=root_b[:])
        nc.gpsimd.tensor_tensor(root_lo[:], root[:], root_hi[:], ALU.subtract)
        diag_x = keep_tile([P, 4, P], BF16, "diag_x")
        diag_z = keep_tile([P, 2, 4, P], BF16, "diag_z")
        sign = keep_tile([P, 8], F32, "sign")
        c_abs = keep_tile([P, 8], F32, "c_abs")
        ln_in = keep_tile([P, 2, 8], F32, "ln_in")
        ln_out = keep_tile([P, 2, 8], F32, "ln_out")
        c_rec = keep_tile([P, 8], F32, "c_rec")
        offset = keep_tile([P, 8], F32, "offset")
        scale = keep_tile([P, 8], F32, "scale")
        c_flat = c_b[:].rearrange("p g t -> p (g t)")

        def c_chain():
            nc.vector.tensor_scalar(sign[:], c_flat, 0.0, 2.0, ALU.is_ge, ALU.mult)
            nc.vector.tensor_scalar(sign[:], sign[:], -1.0, None, ALU.add)
            nc.vector.tensor_tensor(c_abs[:], c_flat, sign[:], ALU.mult)
            nc.vector.tensor_scalar(ln_in[:, 0, :], c_abs[:], LN_LOW, LN_HIGH, ALU.max, ALU.min)
            nc.vector.reciprocal(c_rec[:], ln_in[:, 0, :])
            nc.vector.tensor_tensor(c_rec[:], c_abs[:], c_rec[:], ALU.mult)
            nc.vector.tensor_scalar(ln_in[:, 1, :], c_rec[:], LN_LOW, 2.0 * LN_HIGH, ALU.max, ALU.min)

        def logs():
            nc.gpsimd.tensor_tensor(scale[:], scale_in[:].rearrange("p g t -> p (g t)"), sign[:], ALU.mult)
            nc.scalar.activation(ln_out[:], ln_in[:], ACT.Ln)
            nc.scalar.activation(warm[:], one[:], ACT.Exp)
            nc.gpsimd.tensor_tensor(offset[:], ln_out[:, 0, :], ln_out[:, 1, :], ALU.add)
            nc.gpsimd.tensor_scalar(offset[:], offset[:], -DIST_SCALE / 2, -DIST_SCALE / 2 * LOG_AMPLITUDE, ALU.mult, ALU.add)

        turned, codes, planes = {}, {}, {}
        for kind in "zx":
            turned[kind] = keep_tile([P, 1024, 4], BF16, "turned_" + kind)
            codes[kind] = keep_tile([P, 1024], U32, "codes_" + kind)
            planes[kind] = keep_tile([P, 1024], U8, "planes_" + kind)
        nz = keep_tile([P, 8], F32, "nz")
        nz_half = keep_tile([P, 8], F32, "nz_half")
        junk_s = keep_tile([P, D], BF16, "junk_s")
        junk_v = keep_tile([P, D], BF16, "junk_v")
        nx_col = keep_tile([P, 8], F32, "nx_col")
        nx = keep_tile([P, Q], F32, "nx")
        bq = keep_tile([P, T], U32, "bq")
        bs = keep_tile([P, T], U8, "bs")
        aq = [keep_tile([P, T], U32, f"aq{g}") for g in range(2)]
        a_s = [keep_tile([P, T], U8, f"as{g}") for g in range(2)]
        bank, sq, wide, mixed, dist, kern, kq, ks = {}, {}, {}, {}, {}, {}, {}, {}
        out_view = out.rearrange("(h m j) w -> h j m w", m=P, j=4)

        def move(engine, dst, src):
            if engine == "V":
                nc.vector.tensor_copy(out=dst, in_=src)
            else:
                nc.scalar.copy(dst, src)

        def cols(b, n=256):
            return slice(n * b, n * b + n)

        def mm(o, l, ls, r, rs, start, stop):
            nc.tensor.matmul_mx(out=o, lhsT=l.bitcast(FP8X4), lhsT_scale=ls, rhs=r.bitcast(FP8X4), rhs_scale=rs, start=start, stop=stop)

        def mix(dst, src):
            nc.vector.tensor_copy(out=dst.rearrange("p (n i) t -> p n t i", i=4), in_=src.rearrange("p t (n i) -> p n t i", i=4))

        for step in ORDER.split():
            name, e = step.split(":")
            o = name[0]
            if o == "T":
                k, b = name[1], int(name[2])
                t = psum.tile([P, 2, 2, P], F32, tag="w", bufs=4)
                for r in range(2):
                    view = rows[k, b][:, r, :].bitcast(F32)
                    for u in range(2):
                        nc.tensor.transpose(t[:, r, u, :], view[:, u : D // 2 : 2], ident[:])
                bank["T", k, b] = t
            elif o == "C":
                k, b = name[1], int(name[2])
                move(e, turned[k][:, cols(b), :].bitcast(F32).rearrange("p (r m) u -> p r m u", m=P), bank["T", k, b][:].rearrange("p r u m -> p r m u"))
            elif name == "ZC":
                c_chain()
            elif name == "LN":
                logs()
            elif name == "DX":
                for t in range(4):
                    nc.vector.tensor_scalar(diag_x[:, t, :], ident_b[:], lam_b[:, t : t + 1], None, ALU.mult)
            elif name == "DZ":
                for v, part in enumerate((root_hi, root_lo)):
                    for t in range(4):
                        nc.vector.tensor_scalar(diag_z[:, v, t, :], ident_b[:], part[:, t : t + 1], None, ALU.mult)
            elif o == "Q" and name[1] in "xz":
                k, b = name[1], int(name[2])
                nc.vector.quantize_mx(out=codes[k][:, cols(b)].bitcast(FP8X4), scales=planes[k][:, cols(b)], in_=turned[k][:, cols(b), :].rearrange("p n t -> p (n t)"))
            elif o == "Y":
                k, b, r = name[1], int(name[2]), int(name[3])
                y = psum.tile([P, 4, P], F32, tag="w", bufs=4)
                for t in range(4):
                    left = turned[k][:, 256 * b + P * r : 256 * b + P * r + P, t]
                    if k == "x":
                        nc.tensor.matmul(y[:, t, :], lhsT=left, rhs=diag_x[:, t, :], start=True, stop=True)
                    else:
                        for v in range(2):
                            nc.tensor.matmul(y[:, t, :], lhsT=left, rhs=diag_z[:, v, t, :], start=(v == 0), stop=(v == 1))
                bank["Y", k, b, r] = y
            elif o == "A":
                k, b, r = name[1], int(name[2]), int(name[3])
                y = bank["Y", k, b, r]
                j = 2 * b + r
                if k == "z":
                    nc.scalar.activation(junk_s[:], y[:].rearrange("p t n -> p (t n)"), ACT.Square, accum_out=nz_half[:, j : j + 1])
                else:
                    nc.vector.scalar_tensor_tensor(
                        junk_v[:].rearrange("p (t n) -> p t n", t=4),
                        y[:],
                        0.5,
                        rows[k, b][:, r, :].rearrange("p (n t) -> p t n", t=4),
                        ALU.mult,
                        ALU.mult,
                        accum_out=nx_col[:, j : j + 1],
                    )
            elif o == "F":
                b = int(name[2])
                nc.vector.tensor_tensor(nz[:, cols(b, 2)], nz_half[:, cols(b, 2)], offset[:, cols(b, 2)], ALU.add)
            elif o == "B":
                b = int(name[2])
                t = psum.tile([P, HALF], F32, tag="w", bufs=4)
                for j in range(2):
                    nc.tensor.transpose(t[:, P * j : P * j + P], nx_col[:, 2 * b + j : 2 * b + j + 1].to_broadcast([P, P]), ident[:])
                bank["B", b] = t
            elif o == "X":
                b = int(name[2])
                move(e, nx[:, cols(b)], bank["B", b][:, 0:256])
            elif name[:2] == "MB":
                w = int(name[2])
                mixed["b", w] = keep_tile([P, HALF, 4], BF16, f"mixb{w}")
                v = beta_rows[:, :, cols(w, HALF)]
                mix(mixed["b", w][:], v)
            elif name[:2] == "QB":
                w = int(name[2])
                s = cols(w, HALF)
                nc.vector.quantize_mx(out=bq[:, s].bitcast(FP8X4), scales=bs[:, s], in_=mixed["b", w][:].rearrange("p n t -> p (n t)"))
            elif name[:2] == "WA":
                g, w, k = int(name[2]), int(name[3]), int(name[4])
                if (g, w) not in wide:
                    wide[g, w] = keep_tile([P, 4, HALF], BF16, f"wide{g}{w}")
                for j in (2 * k, 2 * k + 1):
                    v = code_rows[g][:, j, cols(w, HALF)].bitcast(FP8)
                    one_col = scale[:, 4 * g + j : 4 * g + j + 1]
                    if e == "V":
                        nc.vector.tensor_scalar(wide[g, w][:, j, :], v, one_col, None, ALU.mult)
                    else:
                        nc.scalar.activation(wide[g, w][:, j, :], v, ACT.Copy, scale=one_col)
            elif name[:2] == "MA":
                g, w = int(name[2]), int(name[3])
                mixed[g, w] = keep_tile([P, HALF, 4], BF16, f"mix{g}{w}")
                mix(mixed[g, w][:], wide[g, w][:])
            elif name[:2] == "QA":
                g, w = int(name[2]), int(name[3])
                s = cols(w, HALF)
                nc.vector.quantize_mx(out=aq[g][:, s].bitcast(FP8X4), scales=a_s[g][:, s], in_=mixed[g, w][:].rearrange("p n t -> p (n t)"))
            elif o == "D":
                i, g, t0 = int(name[1]), int(name[2]), int(name[3])
                q0, width = CHUNKS[i]
                t = psum.tile([P, HALF], F32, tag="w", bufs=4)
                for s in range(HALF // width):
                    zc = cols(4 * g + t0 + s, P)
                    qc = slice(q0, q0 + width)
                    mm(t[:, cols(s, width)], codes["z"][:, zc], planes["z"][:, zc], codes["x"][:, qc], planes["x"][:, qc], True, True)
                bank["D", i, g, t0] = t
            elif o == "f":
                i, g, t0 = int(name[1]), int(name[2]), int(name[3])
                q0, width = CHUNKS[i]
                if (i, g) not in dist:
                    dist[i, g] = keep_tile([P, 4, width], F32, f"dist{i}{g}")
                for s in range(HALF // width):
                    j = 4 * g + t0 + s
                    nc.vector.scalar_tensor_tensor(dist[i, g][:, t0 + s, :], bank["D", i, g, t0][:, cols(s, width)], nz[:, j : j + 1], nx[:, q0 : q0 + width], ALU.subtract, ALU.subtract)
            elif o == "E":
                i, g = int(name[1]), int(name[2])
                kern[i, g] = keep_tile([P, CHUNKS[i][1], 4], BF16, f"kern{i}{g}")
                nc.scalar.activation(kern[i, g][:].rearrange("p (n i) t -> p n t i", i=4), dist[i, g][:].rearrange("p t (n i) -> p n t i", i=4), ACT.Exp, scale=2.0 / DIST_SCALE)
            elif o == "K":
                i, g = int(name[1]), int(name[2])
                width = CHUNKS[i][1]
                kq[i, g] = keep_tile([P, width], U32, f"kq{i}{g}")
                ks[i, g] = keep_tile([P, width], U8, f"ks{i}{g}")
                nc.vector.quantize_mx(out=kq[i, g][:].bitcast(FP8X4), scales=ks[i, g][:], in_=kern[i, g][:].rearrange("p n t -> p (n t)"))
            else:
                i, b, w = int(name[1]), int(name[2]), int(name[3])
                q0 = CHUNKS[i][0] + P * b
                s = cols(w, HALF)
                if o == "L":
                    t = psum.tile([P, HALF], F32, tag="acc", bufs=4)
                    bank["A", i, b, w] = t
                    qc = slice(q0, q0 + P)
                    mm(t[:], codes["x"][:, qc], planes["x"][:, qc], bq[:, s], bs[:, s], True, False)
                elif o in "GH":
                    g = "GH".index(o)
                    mm(bank["A", i, b, w][:], kq[i, g][:, cols(b, P)], ks[i, g][:, cols(b, P)], aq[g][:, s], a_s[g][:, s], False, g == 1)
                else:
                    t = outs.tile([P, HALF], F32, tag="res")
                    move(e, t[:], bank["A", i, b, w][:])
                    nc.sync.dma_start(out=out_view[q0 // HALF, (q0 % HALF) // P, :, s], in_=t[:])
